import numpy as np
import ml_dtypes


def mxq(x, axis, fmt="e4m3"):
    dtype, down = {"e4m3": (ml_dtypes.float8_e4m3fn, 7), "e5m2": (ml_dtypes.float8_e5m2, 14)}[fmt]
    v = np.moveaxis(np.asarray(x, np.float32).astype(ml_dtypes.bfloat16).astype(np.float64), axis, -1)
    blocks = v.reshape(v.shape[:-1] + (-1, 32))
    amax = np.abs(blocks).max(-1, keepdims=True)
    byte = np.maximum(np.where(amax > 0, np.frexp(amax)[1] - 1 + 127, 0) - down, 1)
    scale = np.exp2(byte - 127.0)
    codes = (blocks / scale).astype(np.float32).astype(dtype).astype(np.float64)
    return np.moveaxis((codes * scale).reshape(v.shape), -1, axis)


WIDE = False


def mx_kscale(k):
    if not WIDE:
        return np.ones(k)
    levels = np.array([30, -30])
    if k % 512:
        return np.exp2(np.random.permutation(np.resize(levels, k // 32))).repeat(32)
    a = np.empty((k // 512, 16))
    for p in range(k // 512):
        a[p, :8] = np.random.permutation(np.resize(levels, 8))
        for g in range(8):
            far = levels[np.abs(levels - a[p, g]) >= 10]
            a[p, g + 8] = far[np.random.randint(len(far))]
    return np.exp2(a.ravel()).repeat(32)


def f64(x):
    return np.asarray(x).astype(np.float64)


def striped(idx):
    return np.tile(np.asarray(idx).reshape(-1, 16).T, (8, 1)).astype(np.uint16)


def unstriped(offs):
    return offs[:16].T.reshape(-1).astype(np.int64)


E2M1 = np.array([0.0, 0.5, 1.0, 1.5, 2.0, 3.0, 4.0, 6.0, -0.0, -0.5, -1.0, -1.5, -2.0, -3.0, -4.0, -6.0])


def pack_weight(w, fmt):
    k, n = w.shape
    w = f64(np.asarray(w, np.float32).astype(ml_dtypes.bfloat16)).reshape(k // 32, 32, n)
    amax = np.abs(w).max(1)
    if fmt in ("e4m3", "e5m2"):
        byte = np.frexp(amax)[1] - 1 + 127 - (7 if fmt == "e4m3" else 14)
    else:
        mant, ex = np.frexp(amax / 6.0)
        byte = np.where(mant > 0.5, ex, ex - 1) + 127
    byte = np.clip(np.where(amax > 0, byte, 1), 1, 254)
    scaled = (w * np.exp2(127.0 - byte)[:, None, :]).reshape(k, n).astype(np.float32)
    by_word = np.ascontiguousarray(scaled.reshape(k // 512, 128, 4, n).transpose(0, 1, 3, 2))
    if fmt in ("e4m3", "e5m2"):
        words = by_word.astype(ml_dtypes.float8_e4m3fn if fmt == "e4m3" else ml_dtypes.float8_e5m2).view(np.uint8)
    else:
        c = by_word.astype(ml_dtypes.float4_e2m1fn).view(np.uint8) & 0xF
        words = (c[..., 0::2] | (c[..., 1::2] << 4)).reshape(k // 512, 128, 2 * n)
    return np.ascontiguousarray(words), np.ascontiguousarray(byte.astype(np.uint8).reshape(k // 512, 16, n))


def unpack_weight(words, scales, fmt):
    g, _, n = scales.shape
    words = np.ascontiguousarray(words).reshape(g, 128, n, -1)
    if fmt in ("e4m3", "e5m2"):
        vals = words.view(ml_dtypes.float8_e4m3fn if fmt == "e4m3" else ml_dtypes.float8_e5m2).astype(np.float64)
    else:
        nib = np.empty((g, 128, n, 4), np.uint8)
        nib[..., 0::2] = words & 0xF
        nib[..., 1::2] = words >> 4
        vals = E2M1[nib]
    vals = vals * np.repeat(np.exp2(scales.astype(np.float64) - 127.0), 8, axis=1)[..., None]
    return vals.transpose(0, 1, 3, 2).reshape(g * 512, n)


K, T, J, I, R, G = 512, 512, 256, 256, 512, 32


def setup_inputs():
    n = np.random.standard_normal
    idx = np.random.permutation(T)[:J]
    idx2 = np.random.permutation(T)[:I]
    fk = mx_kscale(K)
    fr = mx_kscale(R)
    xtp = pack_weight(n((K, T)) / fk[:, None], "e5m2")
    wap = pack_weight(n((K, R)) * 0.5 / np.sqrt(K) * fk[:, None] * fr, "e2m1")
    wbp = pack_weight(n((K, R)) * 1 / np.sqrt(K) * fk[:, None] / fr, "e2m1")
    return {
        "xt_words": xtp[0],
        "xt_scales": xtp[1],
        "wa_words": wap[0],
        "wa_scales": wap[1],
        "wb_words": wbp[0],
        "wb_scales": wbp[1],
        "offs": striped(idx),
        "offs2": striped(idx2),
    }


def reference(xt_words, xt_scales, wa_words, wa_scales, wb_words, wb_scales, offs, offs2):
    idx = unstriped(offs)
    idx2 = unstriped(offs2)
    xtu = unpack_weight(xt_words, xt_scales, "e5m2")
    wau = unpack_weight(wa_words, wa_scales, "e2m1")
    wbu = unpack_weight(wb_words, wb_scales, "e2m1")
    xtidxg = xtu[:, idx]
    za = wau.T @ xtidxg
    ha = np.maximum(za, 0.0)
    xtidx2g = xtu[:, idx2]
    zb = wbu.T @ xtidx2g
    mb1 = zb.reshape(R, G, I // G).mean(axis=2)
    mb2 = np.repeat(mb1, I // G, axis=1)
    hb = zb - mb2
    haq = mxq(ha, 0, "e5m2")
    hbq = mxq(hb, 0, "e5m2")
    a0 = haq.T @ hbq
    a1 = np.pad(a0, ((0, 0), (1, 0)))[:, :I]
    y = 0.04 * np.abs(a0 - a1)
    return y

@@ -1,0 +1,173 @@
+from contextlib import ExitStack
+
+import concourse.mybir as mybir
+
+K, T, J, I, R, BUNDLE = 512, 512, 256, 256, 512, 8
+FLOPS = 2 * K * R * J + 2 * K * R * I + 2 * R * J * I
+
+F32 = mybir.dt.float32
+BF16 = mybir.dt.bfloat16
+I32 = mybir.dt.int32
+U32 = mybir.dt.uint32
+U16 = mybir.dt.uint16
+U8 = mybir.dt.uint8
+E5M2 = mybir.dt.float8_e5m2_x4
+E2M1 = mybir.dt.float4_e2m1fn_x4
+ALU = mybir.AluOpType
+ACT = mybir.ActivationFunctionType
+
+P = 128
+PACK = 4
+HALF = 128
+
+
+def load_scale_rows(queues, plane, scales):
+    for quad in range(4):
+        queues[quad].dma_start(
+            out=plane[32 * quad : 32 * quad + 4, :].bitcast(I32),
+            in_=scales[0, 4 * quad : 4 * quad + 4, :].bitcast(I32),
+        )
+
+
+def deal(nc, dealt, raw):
+    nc.scalar.copy(
+        out=dealt.bitcast(U32).rearrange("p (t q w) -> p t q w", t=PACK, q=16),
+        in_=raw.bitcast(U32).rearrange("p (q t w) -> p t q w", t=PACK, q=16),
+    )
+
+
+def tile_list_meet_plain_levelled_steps_kernel(
+    tc, xt_words, xt_scales, wa_words, wa_scales, wb_words, wb_scales, offs, offs2, out
+):
+    nc = tc.nc
+    with ExitStack() as ctx:
+        sb = ctx.enter_context(tc.tile_pool(name="sb", bufs=1))
+        ps = ctx.enter_context(tc.psum_pool(name="ps", bufs=1))
+
+        row_list = sb.tile([P, J // 16], U16, name="row_list")
+        col_list = sb.tile([P, I // 16], U16, name="col_list")
+        xt_w = sb.tile([P, T], U32, name="xt_w", align_bytes=64)
+        xt_s = sb.tile([P, T], U8, name="xt_s", align_bytes=64)
+        wa_w_raw = sb.tile([P, 2 * R], U8, name="wa_w_raw", align_bytes=64)
+        wb_w_raw = sb.tile([P, 2 * R], U8, name="wb_w_raw", align_bytes=64)
+        wa_s_raw = sb.tile([P, R], U8, name="wa_s_raw", align_bytes=64)
+        wb_s_raw = sb.tile([P, R], U8, name="wb_s_raw", align_bytes=64)
+        wa_w = sb.tile([P, 2 * R], U8, name="wa_w", align_bytes=64)
+        wb_w = sb.tile([P, 2 * R], U8, name="wb_w", align_bytes=64)
+        wa_s = sb.tile([P, R], U8, name="wa_s", align_bytes=64)
+        wb_s = sb.tile([P, R], U8, name="wb_s", align_bytes=64)
+        xa_w = sb.tile([P, J], U32, name="xa_w", align_bytes=64)
+        xa_s = sb.tile([P, J], U8, name="xa_s", align_bytes=64)
+        xb_w = sb.tile([P, I], U32, name="xb_w", align_bytes=64)
+        xb_s = sb.tile([P, I], U8, name="xb_s", align_bytes=64)
+
+        nc.gpsimd.memset(xt_s[:].bitcast(I32), 0)
+        nc.gpsimd.memset(wb_s_raw[:].bitcast(I32), 0)
+        nc.gpsimd.memset(wa_s_raw[:].bitcast(I32), 0)
+
+        nc.sync.dma_start(col_list[:], offs2)
+        nc.sync.dma_start(
+            out=xt_w[:].bitcast(I32),
+            in_=xt_words[0].rearrange("p n t -> p (n t)").bitcast(I32),
+        )
+        load_scale_rows([nc.scalar] * 4, xt_s, xt_scales)
+        nc.sync.dma_start(row_list[:], offs)
+        nc.sync.dma_start(out=wb_w_raw[:].bitcast(I32), in_=wb_words[0].bitcast(I32))
+        nc.gpsimd.dma_start(out=wa_w_raw[:].bitcast(I32), in_=wa_words[0].bitcast(I32))
+        load_scale_rows([nc.sync] * 4, wb_s_raw, wb_scales)
+        load_scale_rows([nc.sync] * 4, wa_s_raw, wa_scales)
+
+        nc.vector.tensor_copy(xb_w[:], xt_w[:].indirect(col_list[:]))
+        nc.vector.tensor_copy(xb_s[:], xt_s[:].indirect(col_list[:]))
+        nc.vector.tensor_copy(xa_w[:], xt_w[:].indirect(row_list[:]))
+        nc.vector.tensor_copy(xa_s[:], xt_s[:].indirect(row_list[:]))
+
+        deal(nc, wb_w[:], wb_w_raw[:])
+        deal(nc, wb_s[:], wb_s_raw[:])
+        deal(nc, wa_w[:], wa_w_raw[:])
+        deal(nc, wa_s[:], wa_s_raw[:])
+
+        def hidden(bank, w_w, w_s, x_w, x_s, half):
+            cols = slice(half * HALF, (half + 1) * HALF)
+            for t in range(PACK):
+                nc.tensor.matmul_mx(
+                    out=bank[:, t, :],
+                    lhsT=w_w[:, 2 * P * t : 2 * P * (t + 1)].bitcast(E2M1),
+                    lhsT_scale=w_s[:, P * t : P * (t + 1)],
+                    rhs=x_w[:, cols].bitcast(E5M2),
+                    rhs_scale=x_s[:, cols],
+                    start=True,
+                    stop=True,
+                )
+
+        zb = [ps.tile([P, PACK, HALF], F32, name=f"zb{h}") for h in range(2)]
+        za = [ps.tile([P, PACK, HALF], F32, name=f"za{h}") for h in range(2)]
+        for h in range(2):
+            hidden(zb[h], wb_w, wb_s, xb_w, xb_s, h)
+        for h in range(2):
+            hidden(za[h], wa_w, wa_s, xa_w, xa_s, h)
+
+        groups = HALF // BUNDLE
+        hb = [sb.tile([P, HALF * PACK], BF16, name=f"hb{h}", align_bytes=64) for h in range(2)]
+        ha = [sb.tile([P, HALF * PACK], BF16, name=f"ha{h}", align_bytes=64) for h in range(2)]
+        sums = [sb.tile([P, groups * PACK], F32, name=f"sums{h}") for h in range(2)]
+        means = [sb.tile([P, groups * PACK], F32, name=f"means{h}") for h in range(2)]
+        for h in range(2):
+            nc.vector.tensor_reduce(
+                out=sums[h][:].rearrange("p (g t) -> p g t", t=PACK),
+                in_=zb[h][:].rearrange("p t (g e) -> p g t e", e=BUNDLE),
+                axis=mybir.AxisListType.X,
+                op=ALU.add,
+            )
+            nc.gpsimd.tensor_scalar(
+                out=means[h][:], in0=sums[h][:], scalar1=1.0 / BUNDLE, scalar2=0.0,
+                op0=ALU.mult, op1=ALU.add,
+            )
+        for h in range(2):
+            nc.scalar.activation(
+                out=ha[h][:].rearrange("p (n t) -> p n t", t=PACK),
+                in_=za[h][:].rearrange("p t n -> p n t"),
+                func=ACT.Relu,
+            )
+        hb_w = [sb.tile([P, HALF], U32, name=f"hb_w{h}", align_bytes=64) for h in range(2)]
+        hb_s = [sb.tile([P, HALF], U8, name=f"hb_s{h}", align_bytes=64) for h in range(2)]
+        ha_w = [sb.tile([P, HALF], U32, name=f"ha_w{h}", align_bytes=64) for h in range(2)]
+        ha_s = [sb.tile([P, HALF], U8, name=f"ha_s{h}", align_bytes=64) for h in range(2)]
+        before = [sb.tile([P, I + 8], F32, name=f"before{a}") for a in range(2)]
+        y = [sb.tile([P, I], F32, name=f"y{a}") for a in range(2)]
+        for a in range(2):
+            nc.gpsimd.memset(before[a][:, 0:1], 0.0)
+
+        def scores(a, h):
+            c0 = h * HALF
+            a0 = ps.tile([P, HALF], F32, name=f"a0_{a}{h}")
+            nc.tensor.matmul_mx(
+                out=a0[:],
+                lhsT=ha_w[a][:].bitcast(E5M2),
+                lhsT_scale=ha_s[a][:],
+                rhs=hb_w[h][:].bitcast(E5M2),
+                rhs_scale=hb_s[h][:],
+                start=True,
+                stop=True,
+            )
+            nc.scalar.copy(out=before[a][:, c0 + 1 : c0 + 1 + HALF], in_=a0[:])
+            step = sb.tile([P, HALF], F32, name=f"step{a}{h}")
+            nc.vector.tensor_tensor(
+                out=step[:], in0=a0[:], in1=before[a][:, c0 : c0 + HALF], op=ALU.subtract
+            )
+            nc.scalar.activation(out=y[a][:, c0 : c0 + HALF], in_=step[:], func=ACT.Abs, scale=0.04)
+
+        for h in range(2):
+            nc.vector.tensor_tensor(
+                out=hb[h][:].rearrange("p (g e t) -> p g e t", e=BUNDLE, t=PACK),
+                in0=zb[h][:].rearrange("p t (g e) -> p g e t", e=BUNDLE),
+                in1=means[h][:].rearrange("p (g t) -> p g t", t=PACK).unsqueeze(2).to_broadcast([P, groups, BUNDLE, PACK]),
+                op=ALU.subtract,
+            )
+            nc.vector.quantize_mx(out=ha_w[h][:].bitcast(E5M2), scales=ha_s[h][:], in_=ha[h][:])
+            nc.vector.quantize_mx(out=hb_w[h][:].bitcast(E5M2), scales=hb_s[h][:], in_=hb[h][:])
+        for h in range(2):
+            for a in range(2):
+                scores(a, h)
+        for a in range(2):
+            nc.sync.dma_start(out=out[a * P : (a + 1) * P, :], in_=y[a][:])

@@ -164,10 +164,11 @@ def tile_list_meet_plain_levelled_steps_kernel(
                 in1=means[h][:].rearrange("p (g t) -> p g t", t=PACK).unsqueeze(2).to_broadcast([P, groups, BUNDLE, PACK]),
                 op=ALU.subtract,
             )
-            nc.vector.quantize_mx(out=ha_w[h][:].bitcast(E5M2), scales=ha_s[h][:], in_=ha[h][:])
-            nc.vector.quantize_mx(out=hb_w[h][:].bitcast(E5M2), scales=hb_s[h][:], in_=hb[h][:])
+        nc.vector.quantize_mx(out=ha_w[0][:].bitcast(E5M2), scales=ha_s[0][:], in_=ha[0][:])
         for h in range(2):
-            for a in range(2):
-                scores(a, h)
+            nc.vector.quantize_mx(out=hb_w[h][:].bitcast(E5M2), scales=hb_s[h][:], in_=hb[h][:])
+        nc.vector.quantize_mx(out=ha_w[1][:].bitcast(E5M2), scales=ha_s[1][:], in_=ha[1][:])
         for a in range(2):
+            for h in range(2):
+                scores(a, h)
             nc.sync.dma_start(out=out[a * P : (a + 1) * P, :], in_=y[a][:])

from contextlib import ExitStack

import concourse.mybir as mybir

K, T, J, I, R, BUNDLE = 512, 512, 256, 256, 512, 8
FLOPS = 2 * K * R * J + 2 * K * R * I + 2 * R * J * I

F32 = mybir.dt.float32
BF16 = mybir.dt.bfloat16
I32 = mybir.dt.int32
U32 = mybir.dt.uint32
U16 = mybir.dt.uint16
U8 = mybir.dt.uint8
E5M2 = mybir.dt.float8_e5m2_x4
E2M1 = mybir.dt.float4_e2m1fn_x4
ALU = mybir.AluOpType
ACT = mybir.ActivationFunctionType

P = 128
PACK = 4
HALF = 128


def load_scale_rows(queues, plane, scales):
    for quad in range(4):
        queues[quad].dma_start(
            out=plane[32 * quad : 32 * quad + 4, :].bitcast(I32),
            in_=scales[0, 4 * quad : 4 * quad + 4, :].bitcast(I32),
        )


def deal(nc, dealt, raw):
    nc.scalar.copy(
        out=dealt.bitcast(U32).rearrange("p (t q w) -> p t q w", t=PACK, q=16),
        in_=raw.bitcast(U32).rearrange("p (q t w) -> p t q w", t=PACK, q=16),
    )


def tile_list_meet_plain_levelled_steps_kernel(
    tc, xt_words, xt_scales, wa_words, wa_scales, wb_words, wb_scales, offs, offs2, out
):
    nc = tc.nc
    with ExitStack() as ctx:
        sb = ctx.enter_context(tc.tile_pool(name="sb", bufs=1))
        ps = ctx.enter_context(tc.psum_pool(name="ps", bufs=1))

        row_list = sb.tile([P, J // 16], U16, name="row_list")
        col_list = sb.tile([P, I // 16], U16, name="col_list")
        xt_w = sb.tile([P, T], U32, name="xt_w", align_bytes=64)
        xt_s = sb.tile([P, T], U8, name="xt_s", align_bytes=64)
        wa_w_raw = sb.tile([P, 2 * R], U8, name="wa_w_raw", align_bytes=64)
        wb_w_raw = sb.tile([P, 2 * R], U8, name="wb_w_raw", align_bytes=64)
        wa_s_raw = sb.tile([P, R], U8, name="wa_s_raw", align_bytes=64)
        wb_s_raw = sb.tile([P, R], U8, name="wb_s_raw", align_bytes=64)
        wa_w = sb.tile([P, 2 * R], U8, name="wa_w", align_bytes=64)
        wb_w = sb.tile([P, 2 * R], U8, name="wb_w", align_bytes=64)
        wa_s = sb.tile([P, R], U8, name="wa_s", align_bytes=64)
        wb_s = sb.tile([P, R], U8, name="wb_s", align_bytes=64)
        xa_w = sb.tile([P, J], U32, name="xa_w", align_bytes=64)
        xa_s = sb.tile([P, J], U8, name="xa_s", align_bytes=64)
        xb_w = sb.tile([P, I], U32, name="xb_w", align_bytes=64)
        xb_s = sb.tile([P, I], U8, name="xb_s", align_bytes=64)

        nc.gpsimd.memset(xt_s[:].bitcast(I32), 0)
        nc.gpsimd.memset(wb_s_raw[:].bitcast(I32), 0)
        nc.gpsimd.memset(wa_s_raw[:].bitcast(I32), 0)

        nc.sync.dma_start(col_list[:], offs2)
        nc.sync.dma_start(
            out=xt_w[:].bitcast(I32),
            in_=xt_words[0].rearrange("p n t -> p (n t)").bitcast(I32),
        )
        load_scale_rows([nc.scalar] * 4, xt_s, xt_scales)
        nc.sync.dma_start(row_list[:], offs)
        nc.sync.dma_start(out=wb_w_raw[:].bitcast(I32), in_=wb_words[0].bitcast(I32))
        nc.gpsimd.dma_start(out=wa_w_raw[:].bitcast(I32), in_=wa_words[0].bitcast(I32))
        load_scale_rows([nc.sync] * 4, wb_s_raw, wb_scales)
        load_scale_rows([nc.sync] * 4, wa_s_raw, wa_scales)

        nc.vector.tensor_copy(xb_w[:], xt_w[:].indirect(col_list[:]))
        nc.vector.tensor_copy(xb_s[:], xt_s[:].indirect(col_list[:]))
        nc.vector.tensor_copy(xa_w[:], xt_w[:].indirect(row_list[:]))
        nc.vector.tensor_copy(xa_s[:], xt_s[:].indirect(row_list[:]))

        deal(nc, wb_w[:], wb_w_raw[:])
        deal(nc, wb_s[:], wb_s_raw[:])
        deal(nc, wa_w[:], wa_w_raw[:])
        deal(nc, wa_s[:], wa_s_raw[:])

        def hidden(bank, w_w, w_s, x_w, x_s, half):
            cols = slice(half * HALF, (half + 1) * HALF)
            for t in range(PACK):
                nc.tensor.matmul_mx(
                    out=bank[:, t, :],
                    lhsT=w_w[:, 2 * P * t : 2 * P * (t + 1)].bitcast(E2M1),
                    lhsT_scale=w_s[:, P * t : P * (t + 1)],
                    rhs=x_w[:, cols].bitcast(E5M2),
                    rhs_scale=x_s[:, cols],
                    start=True,
                    stop=True,
                )

        zb = [ps.tile([P, PACK, HALF], F32, name=f"zb{h}") for h in range(2)]
        za = [ps.tile([P, PACK, HALF], F32, name=f"za{h}") for h in range(2)]
        for h in range(2):
            hidden(zb[h], wb_w, wb_s, xb_w, xb_s, h)
        for h in range(2):
            hidden(za[h], wa_w, wa_s, xa_w, xa_s, h)

        groups = HALF // BUNDLE
        hb = [sb.tile([P, HALF * PACK], BF16, name=f"hb{h}", align_bytes=64) for h in range(2)]
        ha = [sb.tile([P, HALF * PACK], BF16, name=f"ha{h}", align_bytes=64) for h in range(2)]
        sums = [sb.tile([P, groups * PACK], F32, name=f"sums{h}") for h in range(2)]
        means = [sb.tile([P, groups * PACK], F32, name=f"means{h}") for h in range(2)]
        for h in range(2):
            nc.vector.tensor_reduce(
                out=sums[h][:].rearrange("p (g t) -> p g t", t=PACK),
                in_=zb[h][:].rearrange("p t (g e) -> p g t e", e=BUNDLE),
                axis=mybir.AxisListType.X,
                op=ALU.add,
            )
            nc.gpsimd.tensor_scalar(
                out=means[h][:], in0=sums[h][:], scalar1=1.0 / BUNDLE, scalar2=0.0,
                op0=ALU.mult, op1=ALU.add,
            )
        for h in range(2):
            nc.scalar.activation(
                out=ha[h][:].rearrange("p (n t) -> p n t", t=PACK),
                in_=za[h][:].rearrange("p t n -> p n t"),
                func=ACT.Relu,
            )
        hb_w = [sb.tile([P, HALF], U32, name=f"hb_w{h}", align_bytes=64) for h in range(2)]
        hb_s = [sb.tile([P, HALF], U8, name=f"hb_s{h}", align_bytes=64) for h in range(2)]
        ha_w = [sb.tile([P, HALF], U32, name=f"ha_w{h}", align_bytes=64) for h in range(2)]
        ha_s = [sb.tile([P, HALF], U8, name=f"ha_s{h}", align_bytes=64) for h in range(2)]
        before = [sb.tile([P, I + 8], F32, name=f"before{a}") for a in range(2)]
        y = [sb.tile([P, I], F32, name=f"y{a}") for a in range(2)]
        for a in range(2):
            nc.gpsimd.memset(before[a][:, 0:1], 0.0)

        def scores(a, h):
            c0 = h * HALF
            a0 = ps.tile([P, HALF], F32, name=f"a0_{a}{h}")
            nc.tensor.matmul_mx(
                out=a0[:],
                lhsT=ha_w[a][:].bitcast(E5M2),
                lhsT_scale=ha_s[a][:],
                rhs=hb_w[h][:].bitcast(E5M2),
                rhs_scale=hb_s[h][:],
                start=True,
                stop=True,
            )
            nc.scalar.copy(out=before[a][:, c0 + 1 : c0 + 1 + HALF], in_=a0[:])
            step = sb.tile([P, HALF], F32, name=f"step{a}{h}")
            nc.vector.tensor_tensor(
                out=step[:], in0=a0[:], in1=before[a][:, c0 : c0 + HALF], op=ALU.subtract
            )
            nc.scalar.activation(out=y[a][:, c0 : c0 + HALF], in_=step[:], func=ACT.Abs, scale=0.04)

        for h in range(2):
            nc.vector.tensor_tensor(
                out=hb[h][:].rearrange("p (g e t) -> p g e t", e=BUNDLE, t=PACK),
                in0=zb[h][:].rearrange("p t (g e) -> p g e t", e=BUNDLE),
                in1=means[h][:].rearrange("p (g t) -> p g t", t=PACK).unsqueeze(2).to_broadcast([P, groups, BUNDLE, PACK]),
                op=ALU.subtract,
            )
        nc.vector.quantize_mx(out=ha_w[0][:].bitcast(E5M2), scales=ha_s[0][:], in_=ha[0][:])
        for h in range(2):
            nc.vector.quantize_mx(out=hb_w[h][:].bitcast(E5M2), scales=hb_s[h][:], in_=hb[h][:])
        nc.vector.quantize_mx(out=ha_w[1][:].bitcast(E5M2), scales=ha_s[1][:], in_=ha[1][:])
        for a in range(2):
            for h in range(2):
                scores(a, h)
            nc.sync.dma_start(out=out[a * P : (a + 1) * P, :], in_=y[a][:])
